import numpy as np
import ml_dtypes


def mxq(x, axis, fmt="e4m3"):
    dtype, down = {"e4m3": (ml_dtypes.float8_e4m3fn, 7), "e5m2": (ml_dtypes.float8_e5m2, 14)}[fmt]
    v = np.moveaxis(np.asarray(x, np.float32).astype(ml_dtypes.bfloat16).astype(np.float64), axis, -1)
    blocks = v.reshape(v.shape[:-1] + (-1, 32))
    amax = np.abs(blocks).max(-1, keepdims=True)
    byte = np.maximum(np.where(amax > 0, np.frexp(amax)[1] - 1 + 127, 0) - down, 1)
    scale = np.exp2(byte - 127.0)
    codes = (blocks / scale).astype(np.float32).astype(dtype).astype(np.float64)
    return np.moveaxis((codes * scale).reshape(v.shape), -1, axis)


WIDE = False


def mx_kscale(k):
    if not WIDE:
        return np.ones(k)
    levels = np.array([10, -10, 5, -5, 0])
    if k % 512:
        return np.exp2(np.random.permutation(np.resize(levels, k // 32))).repeat(32)
    a = np.empty((k // 512, 16))
    for p in range(k // 512):
        a[p, :8] = np.random.permutation(np.resize(levels, 8))
        for g in range(8):
            far = levels[np.abs(levels - a[p, g]) >= 10]
            a[p, g + 8] = far[np.random.randint(len(far))]
    return np.exp2(a.ravel()).repeat(32)


def f64(x):
    return np.asarray(x).astype(np.float64)


def striped(idx):
    return np.tile(idx.reshape(-1, 16).T, (8, 1)).astype(np.uint16)


def unstriped(offs):
    return offs[:16].T.reshape(-1).astype(np.int64)


def pack_weight(w):
    k, n = w.shape
    w = f64(np.asarray(w, np.float32).astype(ml_dtypes.bfloat16)).reshape(k // 32, 32, n)
    amax = np.abs(w).max(1)
    byte = np.clip(np.where(amax > 0, np.frexp(amax)[1] - 1 + 127 - 7, 1), 1, 254)
    scaled = (w * np.exp2(127.0 - byte)[:, None, :]).reshape(k, n).astype(np.float32)
    words = np.ascontiguousarray(scaled.reshape(k // 512, 128, 4, n).transpose(0, 1, 3, 2)).astype(ml_dtypes.float8_e4m3fn).view(np.uint8)
    return words, np.ascontiguousarray(byte.astype(np.uint8).reshape(k // 512, 16, n))


def unpack_weight(words, scales):
    g, p, n, _ = words.shape
    vals = np.ascontiguousarray(words).view(ml_dtypes.float8_e4m3fn).astype(np.float64) * np.repeat(np.exp2(scales.astype(np.float64) - 127.0), 8, axis=1)[..., None]
    return vals.transpose(0, 1, 3, 2).reshape(g * 512, n)


K, T, E, C, N = 2048, 512, 8, 128, 256


def by_expert(wq, xq):
    return np.concatenate([wq[e].T @ xq[:, e * C:(e + 1) * C] for e in range(E)], axis=1)


def setup_inputs():
    n = np.random.standard_normal
    s = mx_kscale(K)[:, None]
    first = np.random.permutation(np.repeat(np.arange(E), T // E))
    second = (first + 1 + np.random.permutation(np.repeat(np.arange(E - 1), -(-T // (E - 1)))[:T])) % E
    while np.bincount(second, minlength=E).max() != T // E:
        load = np.bincount(second, minlength=E); hi, lo = int(load.argmax()), int(load.argmin())
        t = np.flatnonzero((second == hi) & (first != lo))[0]; second[t] = lo
    slot_token = np.empty(E * C, np.int64); pos = np.empty((2, T), np.int64); fill = np.zeros(E, np.int64)
    place = np.stack([np.random.permutation(C) for _ in range(E)])
    for r, deal in enumerate((first, second)):
        for t in np.random.permutation(T):
            e = deal[t]; j = e * C + place[e, fill[e]]; fill[e] += 1; slot_token[j] = t; pos[r, t] = j
    g = np.random.uniform(0.2, 0.8, T)
    packed = [pack_weight(m) for m in n((E, K, N)) / np.sqrt(K) / s[None]]
    return {
        "xT": (n((K, T)) * s).astype(np.float32),
        "w_words": np.stack([m[0] for m in packed]),
        "w_scales": np.stack([m[1] for m in packed]),
        "gate": np.stack([np.tile(g, (N, 1)), np.tile(1.0 - g, (N, 1))]).astype(np.float32),
        "offs": striped(slot_token),
        "pos1": striped(pos[0]),
        "pos2": striped(pos[1]),
    }


def reference(xT, w_words, w_scales, gate, offs, pos1, pos2):
    idx = unstriped(offs)
    xq = mxq(f64(xT)[:, idx], 0, "e4m3")
    w = np.stack([unpack_weight(w_words[e], w_scales[e]) for e in range(E)])
    y = by_expert(w, xq)
    return f64(gate[0]) * y[:, unstriped(pos1)] + f64(gate[1]) * y[:, unstriped(pos2)]

@@ -1,0 +1,157 @@
+from contextlib import ExitStack
+
+import concourse.mybir as mybir
+
+K, T, E, C, N = 2048, 512, 8, 128, 256
+FLOPS = 2 * K * N * E * C
+
+F32 = mybir.dt.float32
+BF16 = mybir.dt.bfloat16
+I32 = mybir.dt.int32
+U32 = mybir.dt.uint32
+U16 = mybir.dt.uint16
+U8 = mybir.dt.uint8
+FP8X4 = mybir.dt.float8_e4m3fn_x4
+MULT = mybir.AluOpType.mult
+ADD = mybir.AluOpType.add
+
+P = 128
+PACK = 4
+K_PASS = P * PACK
+PASSES = K // K_PASS
+SLOTS = E * C
+BLOCKS = N // P
+
+COARSE = ((0, 24), (24, 48), (48, 64))
+FINE = ((0, 16), (16, 32), (32, 48), (48, 64))
+VECTOR_SHARE = (352, 128, 0, 0)
+SPLIT = 2
+
+
+def tile_routed_moe_kernel(tc, xT, w_words, w_scales, gate, offs, pos1, pos2, out):
+    nc = tc.nc
+    with ExitStack() as ctx:
+        lists = ctx.enter_context(tc.tile_pool(name="lists", bufs=1))
+        keep = ctx.enter_context(tc.tile_pool(name="keep", bufs=1))
+        psum = ctx.enter_context(tc.psum_pool(name="psum", bufs=8))
+
+        offs_t = lists.tile([P, SLOTS // 16], U16, name="offs_t")
+        pos1_t = lists.tile([P, T // 16], U16, name="pos1_t")
+        pos2_t = lists.tile([P, T // 16], U16, name="pos2_t")
+
+        raw = [keep.tile([P, PACK, T], F32, name="raw%d" % a) for a in range(PASSES)]
+        grouped = [keep.tile([P, T, PACK], BF16, name="grouped%d" % a, align_bytes=64) for a in range(PASSES)]
+        tok_words = [keep.tile([P, T], U32, name="tok_words%d" % a, align_bytes=64) for a in range(PASSES)]
+        tok_scales = keep.tile([P, T], U8, name="tok_scales", align_bytes=64)
+        slot_words = keep.tile([P, PASSES, SLOTS], U32, name="slot_words", align_bytes=64)
+        slot_scales = keep.tile([P, SLOTS], U8, name="slot_scales", align_bytes=64)
+        wt_words = [keep.tile([P, PASSES, N], I32, name="wt_words%d" % e, align_bytes=64) for e in range(E)]
+        wt_scales = keep.tile([P, E * PASSES, N], U8, name="wt_scales", align_bytes=64)
+        gates = [[keep.tile([P, T], F32, name="gate%d_%d" % (r, b)) for b in range(BLOCKS)] for r in range(2)]
+        y = [keep.tile([P, SLOTS], F32, name="y%d" % b) for b in range(BLOCKS)]
+
+        warm_in = keep.tile([P, 1], F32, name="warm_in")
+        warm_out = keep.tile([P, 1], F32, name="warm_out")
+        nc.vector.memset(warm_in[:], 0.0)
+        nc.scalar.copy(out=warm_out[:], in_=warm_in[:])
+        nc.gpsimd.memset(tok_scales[:], 0)
+        nc.vector.memset(wt_scales[:].rearrange("p g n -> p (g n)").bitcast(I32), 0)
+
+        for a in range(PASSES):
+            nc.sync.dma_start(
+                out=raw[a][:],
+                in_=xT[a * K_PASS : (a + 1) * K_PASS, :].rearrange("(p j) w -> p j w", j=PACK),
+            )
+            if a == 0:
+                nc.sync.dma_start(offs_t[:], offs)
+        nc.sync.dma_start(pos1_t[:], pos1)
+        nc.sync.dma_start(pos2_t[:], pos2)
+        scale_rows = w_scales.rearrange("e a (q r) n -> r q (e a) n", r=4)
+        for r in range(4):
+            nc.sync.dma_start(out=wt_scales[r:P:32, :, :].bitcast(I32), in_=scale_rows[r].bitcast(I32))
+        for e in range(E - SPLIT):
+            nc.sync.dma_start(
+                out=wt_words[e][:],
+                in_=w_words[e].rearrange("a p n r -> p a (n r)").bitcast(I32),
+            )
+        for b in range(BLOCKS):
+            for e in range(E - SPLIT, E):
+                nc.sync.dma_start(
+                    out=wt_words[e][:, :, b * P : (b + 1) * P],
+                    in_=w_words[e].rearrange("a p n r -> p a (n r)")[:, :, 4 * b * P : 4 * (b + 1) * P].bitcast(I32),
+                )
+            for r in range(2):
+                nc.sync.dma_start(out=gates[r][b][:], in_=gate[r, b * P : (b + 1) * P, :])
+
+        for a in range(PASSES):
+            cut = VECTOR_SHARE[a]
+            for lo, hi, on_vector in ((0, cut, True), (cut, T, False)):
+                if lo < hi:
+                    dst = grouped[a][:, lo:hi, :].rearrange("p (c i) t -> p c t i", i=4)
+                    src = raw[a][:, :, lo:hi].rearrange("p t (c i) -> p c t i", i=4)
+                    if on_vector:
+                        nc.vector.tensor_copy(out=dst, in_=src)
+                    else:
+                        nc.scalar.copy(out=dst, in_=src)
+
+        def quantise(a):
+            nc.vector.quantize_mx(
+                out=tok_words[a][:].bitcast(FP8X4),
+                scales=tok_scales[4 * a : P, :],
+                in_=grouped[a][:].rearrange("p w j -> p (w j)"),
+            )
+
+        def gather_words(a, cols):
+            lo, hi = cols
+            nc.vector.tensor_copy(
+                out=slot_words[:, a, 16 * lo : 16 * hi],
+                in_=tok_words[a][:].indirect(offs_t[:, lo:hi]),
+            )
+
+        def gather_scales(cols):
+            lo, hi = cols
+            nc.vector.tensor_copy(
+                out=slot_scales[:, 16 * lo : 16 * hi],
+                in_=tok_scales[:].indirect(offs_t[:, lo:hi]),
+            )
+
+        for a in range(PASSES - 1):
+            quantise(a)
+            for cols in COARSE:
+                gather_words(a, cols)
+        quantise(PASSES - 1)
+        gather_scales(FINE[0])
+        for i in range(len(FINE)):
+            if i + 1 < len(FINE):
+                gather_scales(FINE[i + 1])
+            gather_words(PASSES - 1, FINE[i])
+
+        whole = [(e, b) for e in range(E - SPLIT) for b in range(BLOCKS)]
+        order = whole + [(e, b) for b in range(BLOCKS) for e in range(E - SPLIT, E)]
+        for e, b in order:
+            slots = slice(e * C, (e + 1) * C)
+            feats = slice(b * P, (b + 1) * P)
+            acc = psum.tile([P, C], F32)
+            for a in range(PASSES):
+                nc.tensor.matmul_mx(
+                    out=acc[:],
+                    lhsT=wt_words[e][:, a, feats].bitcast(FP8X4),
+                    lhsT_scale=wt_scales[:, e * PASSES + a, feats],
+                    rhs=slot_words[:, a, slots].bitcast(FP8X4),
+                    rhs_scale=slot_scales[4 * a : P, slots],
+                    start=(a == 0),
+                    stop=(a == PASSES - 1),
+                )
+            if (e, b) == (E - 1, 0):
+                nc.vector.tensor_copy(out=y[b][:, slots], in_=acc[:])
+            else:
+                nc.scalar.copy(out=y[b][:, slots], in_=acc[:])
+
+        for b in range(BLOCKS):
+            first = keep.tile([P, T], F32, name="first%d" % b)
+            second = keep.tile([P, T], F32, name="second%d" % b)
+            total = keep.tile([P, T], F32, name="total%d" % b)
+            nc.vector.tensor_tensor(out=first[:], in0=y[b][:].indirect(pos1_t[:]), in1=gates[0][b][:], op=MULT)
+            nc.vector.tensor_tensor(out=second[:], in0=y[b][:].indirect(pos2_t[:]), in1=gates[1][b][:], op=MULT)
+            nc.vector.tensor_tensor(out=total[:], in0=first[:], in1=second[:], op=ADD)
+            nc.sync.dma_start(out=out[b * P : (b + 1) * P, :], in_=total[:])

@@ -23,7 +23,6 @@ SLOTS = E * C
 BLOCKS = N // P
 
 COARSE = ((0, 24), (24, 48), (48, 64))
-FINE = ((0, 16), (16, 32), (32, 48), (48, 64))
 VECTOR_SHARE = (352, 128, 0, 0)
 SPLIT = 2
 
@@ -120,14 +119,12 @@ def tile_routed_moe_kernel(tc, xT, w_words, w_scales, gate, offs, pos1, pos2, ou
             for cols in COARSE:
                 gather_words(a, cols)
         quantise(PASSES - 1)
-        gather_scales(FINE[0])
-        for i in range(len(FINE)):
-            if i + 1 < len(FINE):
-                gather_scales(FINE[i + 1])
-            gather_words(PASSES - 1, FINE[i])
+        for cols in COARSE:
+            gather_scales(cols)
+        for cols in COARSE:
+            gather_words(PASSES - 1, cols)
 
-        whole = [(e, b) for e in range(E - SPLIT) for b in range(BLOCKS)]
-        order = whole + [(e, b) for b in range(BLOCKS) for e in range(E - SPLIT, E)]
+        order = [(e, b) for b in range(BLOCKS) for e in range(E)]
         for e, b in order:
             slots = slice(e * C, (e + 1) * C)
             feats = slice(b * P, (b + 1) * P)

@@ -25,6 +25,7 @@ BLOCKS = N // P
 COARSE = ((0, 24), (24, 48), (48, 64))
 VECTOR_SHARE = (352, 128, 0, 0)
 SPLIT = 2
+PLANES = 2
 
 
 def tile_routed_moe_kernel(tc, xT, w_words, w_scales, gate, offs, pos1, pos2, out):
@@ -45,7 +46,7 @@ def tile_routed_moe_kernel(tc, xT, w_words, w_scales, gate, offs, pos1, pos2, ou
         slot_words = keep.tile([P, PASSES, SLOTS], U32, name="slot_words", align_bytes=64)
         slot_scales = keep.tile([P, SLOTS], U8, name="slot_scales", align_bytes=64)
         wt_words = [keep.tile([P, PASSES, N], I32, name="wt_words%d" % e, align_bytes=64) for e in range(E)]
-        wt_scales = keep.tile([P, E * PASSES, N], U8, name="wt_scales", align_bytes=64)
+        wt_scales = keep.tile([P, E * PASSES // PLANES, N], U8, name="wt_scales", align_bytes=64)
         gates = [[keep.tile([P, T], F32, name="gate%d_%d" % (r, b)) for b in range(BLOCKS)] for r in range(2)]
         y = [keep.tile([P, SLOTS], F32, name="y%d" % b) for b in range(BLOCKS)]
 
@@ -56,6 +57,11 @@ def tile_routed_moe_kernel(tc, xT, w_words, w_scales, gate, offs, pos1, pos2, ou
         nc.gpsimd.memset(tok_scales[:], 0)
         nc.vector.memset(wt_scales[:].rearrange("p g n -> p (g n)").bitcast(I32), 0)
 
+        scale_rows = w_scales.rearrange("e (c j) (q r) n -> j r q (e c) n", j=PLANES, r=4)
+        for j in range(PLANES):
+            for r in range(4):
+                nc.gpsimd.dma_start(out=wt_scales[4 * j + r : P : 32, :, :].bitcast(F32), in_=scale_rows[j, r].bitcast(F32))
+
         for a in range(PASSES):
             nc.sync.dma_start(
                 out=raw[a][:],
@@ -65,9 +71,6 @@ def tile_routed_moe_kernel(tc, xT, w_words, w_scales, gate, offs, pos1, pos2, ou
                 nc.sync.dma_start(offs_t[:], offs)
         nc.sync.dma_start(pos1_t[:], pos1)
         nc.sync.dma_start(pos2_t[:], pos2)
-        scale_rows = w_scales.rearrange("e a (q r) n -> r q (e a) n", r=4)
-        for r in range(4):
-            nc.sync.dma_start(out=wt_scales[r:P:32, :, :].bitcast(I32), in_=scale_rows[r].bitcast(I32))
         for e in range(E - SPLIT):
             nc.sync.dma_start(
                 out=wt_words[e][:],
@@ -133,7 +136,7 @@ def tile_routed_moe_kernel(tc, xT, w_words, w_scales, gate, offs, pos1, pos2, ou
                 nc.tensor.matmul_mx(
                     out=acc[:],
                     lhsT=wt_words[e][:, a, feats].bitcast(FP8X4),
-                    lhsT_scale=wt_scales[:, e * PASSES + a, feats],
+                    lhsT_scale=wt_scales[4 * (a % PLANES) : P, (e * PASSES + a) // PLANES, feats],
                     rhs=slot_words[:, a, slots].bitcast(FP8X4),
                     rhs_scale=slot_scales[4 * a : P, slots],
                     start=(a == 0),

@@ -1,6 +1,7 @@
 from contextlib import ExitStack
 
 import concourse.mybir as mybir
+from concourse.masks import make_identity
 
 K, T, E, C, N = 2048, 512, 8, 128, 256
 FLOPS = 2 * K * N * E * C
@@ -62,6 +63,9 @@ def tile_routed_moe_kernel(tc, xT, w_words, w_scales, gate, offs, pos1, pos2, ou
             for r in range(4):
                 nc.gpsimd.dma_start(out=wt_scales[4 * j + r : P : 32, :, :].bitcast(F32), in_=scale_rows[j, r].bitcast(F32))
 
+        ident = keep.tile([P, P], F32, name="ident")
+        make_identity(nc, ident[:])
+
         for a in range(PASSES):
             nc.sync.dma_start(
                 out=raw[a][:],
@@ -117,11 +121,15 @@ def tile_routed_moe_kernel(tc, xT, w_words, w_scales, gate, offs, pos1, pos2, ou
                 in_=tok_scales[:].indirect(offs_t[:, lo:hi]),
             )
 
+        quantise(0)
         for a in range(PASSES - 1):
-            quantise(a)
-            for cols in COARSE:
+            for cols in COARSE[:-1]:
                 gather_words(a, cols)
-        quantise(PASSES - 1)
+            if a >= 1:
+                quantise(a + 1)
+            gather_words(a, COARSE[-1])
+            if a < 1:
+                quantise(a + 1)
         for cols in COARSE:
             gather_scales(cols)
         for cols in COARSE:
@@ -147,11 +155,24 @@ def tile_routed_moe_kernel(tc, xT, w_words, w_scales, gate, offs, pos1, pos2, ou
             else:
                 nc.scalar.copy(out=y[b][:, slots], in_=acc[:])
 
-        for b in range(BLOCKS):
-            first = keep.tile([P, T], F32, name="first%d" % b)
-            second = keep.tile([P, T], F32, name="second%d" % b)
-            total = keep.tile([P, T], F32, name="total%d" % b)
-            nc.vector.tensor_tensor(out=first[:], in0=y[b][:].indirect(pos1_t[:]), in1=gates[0][b][:], op=MULT)
-            nc.vector.tensor_tensor(out=second[:], in0=y[b][:].indirect(pos2_t[:]), in1=gates[1][b][:], op=MULT)
-            nc.vector.tensor_tensor(out=total[:], in0=first[:], in1=second[:], op=ADD)
-            nc.sync.dma_start(out=out[b * P : (b + 1) * P, :], in_=total[:])
+        first = [keep.tile([P, T], F32, name="first%d" % b) for b in range(BLOCKS)]
+        second = [keep.tile([P, T], F32, name="second%d" % b) for b in range(BLOCKS)]
+        total = [keep.tile([P, T], F32, name="total%d" % b) for b in range(BLOCKS)]
+
+        nc.vector.tensor_tensor(out=first[0][:], in0=y[0][:].indirect(pos1_t[:]), in1=gates[0][0][:], op=MULT)
+        nc.vector.tensor_tensor(out=second[0][:], in0=y[0][:].indirect(pos2_t[:]), in1=gates[1][0][:], op=MULT)
+        acc = psum.tile([P, T], F32)
+        nc.tensor.matmul(out=acc[:], lhsT=ident[:], rhs=first[0][:], start=True, stop=False)
+        nc.tensor.matmul(out=acc[:], lhsT=ident[:], rhs=second[0][:], start=False, stop=True)
+        nc.scalar.copy(out=total[0][:], in_=acc[:])
+        nc.sync.dma_start(out=out[0:P, :], in_=total[0][:])
+
+        nc.vector.tensor_tensor(out=first[1][:], in0=y[1][:].indirect(pos1_t[:]), in1=gates[0][1][:], op=MULT)
+        halves = ((0, T // 2), (T // 2, T))
+        for lo, hi in halves:
+            nc.vector.tensor_tensor(
+                out=second[1][:, lo:hi], in0=y[1][:].indirect(pos2_t[:, lo // 16 : hi // 16]), in1=gates[1][1][:, lo:hi], op=MULT
+            )
+        for lo, hi in halves:
+            nc.vector.tensor_tensor(out=total[1][:, lo:hi], in0=first[1][:, lo:hi], in1=second[1][:, lo:hi], op=ADD)
+            nc.sync.dma_start(out=out[P : 2 * P, lo:hi], in_=total[1][:, lo:hi])

@@ -48,7 +48,9 @@ def tile_routed_moe_kernel(tc, xT, w_words, w_scales, gate, offs, pos1, pos2, ou
         slot_scales = keep.tile([P, SLOTS], U8, name="slot_scales", align_bytes=64)
         wt_words = [keep.tile([P, PASSES, N], I32, name="wt_words%d" % e, align_bytes=64) for e in range(E)]
         wt_scales = keep.tile([P, E * PASSES // PLANES, N], U8, name="wt_scales", align_bytes=64)
-        gates = [[keep.tile([P, T], F32, name="gate%d_%d" % (r, b)) for b in range(BLOCKS)] for r in range(2)]
+        gate_rows = keep.tile([P, 2, T], F32, name="gate_rows")
+        ones = keep.tile([P, P], F32, name="ones")
+        gates = [keep.tile([P, T], F32, name="gate%d" % r) for r in range(2)]
         y = [keep.tile([P, SLOTS], F32, name="y%d" % b) for b in range(BLOCKS)]
 
         warm_in = keep.tile([P, 1], F32, name="warm_in")
@@ -56,6 +58,8 @@ def tile_routed_moe_kernel(tc, xT, w_words, w_scales, gate, offs, pos1, pos2, ou
         nc.vector.memset(warm_in[:], 0.0)
         nc.scalar.copy(out=warm_out[:], in_=warm_in[:])
         nc.gpsimd.memset(tok_scales[:], 0)
+        nc.vector.memset(gate_rows[:], 0.0)
+        nc.vector.memset(ones[:], 1.0)
         nc.vector.memset(wt_scales[:].rearrange("p g n -> p (g n)").bitcast(I32), 0)
 
         scale_rows = w_scales.rearrange("e (c j) (q r) n -> j r q (e c) n", j=PLANES, r=4)
@@ -75,6 +79,7 @@ def tile_routed_moe_kernel(tc, xT, w_words, w_scales, gate, offs, pos1, pos2, ou
                 nc.sync.dma_start(offs_t[:], offs)
         nc.sync.dma_start(pos1_t[:], pos1)
         nc.sync.dma_start(pos2_t[:], pos2)
+        nc.sync.dma_start(out=gate_rows[0:1, :, :], in_=gate[:, 0:1, :].rearrange("r o t -> o r t"))
         for e in range(E - SPLIT):
             nc.sync.dma_start(
                 out=wt_words[e][:],
@@ -86,8 +91,6 @@ def tile_routed_moe_kernel(tc, xT, w_words, w_scales, gate, offs, pos1, pos2, ou
                     out=wt_words[e][:, :, b * P : (b + 1) * P],
                     in_=w_words[e].rearrange("a p n r -> p a (n r)")[:, :, 4 * b * P : 4 * (b + 1) * P].bitcast(I32),
                 )
-            for r in range(2):
-                nc.sync.dma_start(out=gates[r][b][:], in_=gate[r, b * P : (b + 1) * P, :])
 
         for a in range(PASSES):
             cut = VECTOR_SHARE[a]
@@ -99,6 +102,11 @@ def tile_routed_moe_kernel(tc, xT, w_words, w_scales, gate, offs, pos1, pos2, ou
                         nc.vector.tensor_copy(out=dst, in_=src)
                     else:
                         nc.scalar.copy(out=dst, in_=src)
+
+        for r in range(2):
+            acc = psum.tile([P, T], F32)
+            nc.tensor.matmul(out=acc[:], lhsT=ones[:], rhs=gate_rows[:, r, :], start=True, stop=True)
+            nc.scalar.copy(out=gates[r][:], in_=acc[:])
 
         def quantise(a):
             nc.vector.quantize_mx(
@@ -159,19 +167,19 @@ def tile_routed_moe_kernel(tc, xT, w_words, w_scales, gate, offs, pos1, pos2, ou
         second = [keep.tile([P, T], F32, name="second%d" % b) for b in range(BLOCKS)]
         total = [keep.tile([P, T], F32, name="total%d" % b) for b in range(BLOCKS)]
 
-        nc.vector.tensor_tensor(out=first[0][:], in0=y[0][:].indirect(pos1_t[:]), in1=gates[0][0][:], op=MULT)
-        nc.vector.tensor_tensor(out=second[0][:], in0=y[0][:].indirect(pos2_t[:]), in1=gates[1][0][:], op=MULT)
+        nc.vector.tensor_tensor(out=first[0][:], in0=y[0][:].indirect(pos1_t[:]), in1=gates[0][:], op=MULT)
+        nc.vector.tensor_tensor(out=second[0][:], in0=y[0][:].indirect(pos2_t[:]), in1=gates[1][:], op=MULT)
         acc = psum.tile([P, T], F32)
         nc.tensor.matmul(out=acc[:], lhsT=ident[:], rhs=first[0][:], start=True, stop=False)
         nc.tensor.matmul(out=acc[:], lhsT=ident[:], rhs=second[0][:], start=False, stop=True)
         nc.scalar.copy(out=total[0][:], in_=acc[:])
         nc.sync.dma_start(out=out[0:P, :], in_=total[0][:])
 
-        nc.vector.tensor_tensor(out=first[1][:], in0=y[1][:].indirect(pos1_t[:]), in1=gates[0][1][:], op=MULT)
+        nc.vector.tensor_tensor(out=first[1][:], in0=y[1][:].indirect(pos1_t[:]), in1=gates[0][:], op=MULT)
         halves = ((0, T // 2), (T // 2, T))
         for lo, hi in halves:
             nc.vector.tensor_tensor(
-                out=second[1][:, lo:hi], in0=y[1][:].indirect(pos2_t[:, lo // 16 : hi // 16]), in1=gates[1][1][:, lo:hi], op=MULT
+                out=second[1][:, lo:hi], in0=y[1][:].indirect(pos2_t[:, lo // 16 : hi // 16]), in1=gates[1][:, lo:hi], op=MULT
             )
         for lo, hi in halves:
             nc.vector.tensor_tensor(out=total[1][:, lo:hi], in0=first[1][:, lo:hi], in1=second[1][:, lo:hi], op=ADD)

@@ -62,11 +62,6 @@ def tile_routed_moe_kernel(tc, xT, w_words, w_scales, gate, offs, pos1, pos2, ou
         nc.vector.memset(ones[:], 1.0)
         nc.vector.memset(wt_scales[:].rearrange("p g n -> p (g n)").bitcast(I32), 0)
 
-        scale_rows = w_scales.rearrange("e (c j) (q r) n -> j r q (e c) n", j=PLANES, r=4)
-        for j in range(PLANES):
-            for r in range(4):
-                nc.gpsimd.dma_start(out=wt_scales[4 * j + r : P : 32, :, :].bitcast(F32), in_=scale_rows[j, r].bitcast(F32))
-
         ident = keep.tile([P, P], F32, name="ident")
         make_identity(nc, ident[:])
 
@@ -80,6 +75,10 @@ def tile_routed_moe_kernel(tc, xT, w_words, w_scales, gate, offs, pos1, pos2, ou
         nc.sync.dma_start(pos1_t[:], pos1)
         nc.sync.dma_start(pos2_t[:], pos2)
         nc.sync.dma_start(out=gate_rows[0:1, :, :], in_=gate[:, 0:1, :].rearrange("r o t -> o r t"))
+        scale_rows = w_scales.rearrange("e (c j) (q r) n -> j r q (e c) n", j=PLANES, r=4)
+        for j in range(PLANES):
+            for r in range(4):
+                nc.sync.dma_start(out=wt_scales[4 * j + r : P : 32, :, :].bitcast(I32), in_=scale_rows[j, r].bitcast(I32))
         for e in range(E - SPLIT):
             nc.sync.dma_start(
                 out=wt_words[e][:],

@@ -72,8 +72,6 @@ def tile_routed_moe_kernel(tc, xT, w_words, w_scales, gate, offs, pos1, pos2, ou
             )
             if a == 0:
                 nc.sync.dma_start(offs_t[:], offs)
-        nc.sync.dma_start(pos1_t[:], pos1)
-        nc.sync.dma_start(pos2_t[:], pos2)
         nc.sync.dma_start(out=gate_rows[0:1, :, :], in_=gate[:, 0:1, :].rearrange("r o t -> o r t"))
         scale_rows = w_scales.rearrange("e (c j) (q r) n -> j r q (e c) n", j=PLANES, r=4)
         for j in range(PLANES):
@@ -84,6 +82,9 @@ def tile_routed_moe_kernel(tc, xT, w_words, w_scales, gate, offs, pos1, pos2, ou
                 out=wt_words[e][:],
                 in_=w_words[e].rearrange("a p n r -> p a (n r)").bitcast(I32),
             )
+            if e == 1:
+                nc.sync.dma_start(pos1_t[:], pos1)
+                nc.sync.dma_start(pos2_t[:], pos2)
         for b in range(BLOCKS):
             for e in range(E - SPLIT, E):
                 nc.sync.dma_start(

@@ -40,7 +40,7 @@ def tile_routed_moe_kernel(tc, xT, w_words, w_scales, gate, offs, pos1, pos2, ou
         pos1_t = lists.tile([P, T // 16], U16, name="pos1_t")
         pos2_t = lists.tile([P, T // 16], U16, name="pos2_t")
 
-        raw = [keep.tile([P, PACK, T], F32, name="raw%d" % a) for a in range(PASSES)]
+        raw = [keep.tile([P, PACK, T], F32, name="raw%d" % a, tag="late" if a == PASSES - 1 else "raw%d" % a) for a in range(PASSES)]
         grouped = [keep.tile([P, T, PACK], BF16, name="grouped%d" % a, align_bytes=64) for a in range(PASSES)]
         tok_words = [keep.tile([P, T], U32, name="tok_words%d" % a, align_bytes=64) for a in range(PASSES)]
         tok_scales = keep.tile([P, T], U8, name="tok_scales", align_bytes=64)
@@ -49,7 +49,6 @@ def tile_routed_moe_kernel(tc, xT, w_words, w_scales, gate, offs, pos1, pos2, ou
         wt_words = [keep.tile([P, PASSES, N], I32, name="wt_words%d" % e, align_bytes=64) for e in range(E)]
         wt_scales = keep.tile([P, E * PASSES // PLANES, N], U8, name="wt_scales", align_bytes=64)
         gate_rows = keep.tile([P, 2, T], F32, name="gate_rows")
-        ones = keep.tile([P, P], F32, name="ones")
         gates = [keep.tile([P, T], F32, name="gate%d" % r) for r in range(2)]
         y = [keep.tile([P, SLOTS], F32, name="y%d" % b) for b in range(BLOCKS)]
 
@@ -59,7 +58,6 @@ def tile_routed_moe_kernel(tc, xT, w_words, w_scales, gate, offs, pos1, pos2, ou
         nc.scalar.copy(out=warm_out[:], in_=warm_in[:])
         nc.gpsimd.memset(tok_scales[:], 0)
         nc.vector.memset(gate_rows[:], 0.0)
-        nc.vector.memset(ones[:], 1.0)
         nc.vector.memset(wt_scales[:].rearrange("p g n -> p (g n)").bitcast(I32), 0)
 
         ident = keep.tile([P, P], F32, name="ident")
@@ -103,6 +101,8 @@ def tile_routed_moe_kernel(tc, xT, w_words, w_scales, gate, offs, pos1, pos2, ou
                     else:
                         nc.scalar.copy(out=dst, in_=src)
 
+        ones = keep.tile([P, P], F32, name="ones", tag="late")
+        nc.gpsimd.memset(ones[:], 1.0)
         for r in range(2):
             acc = psum.tile([P, T], F32)
             nc.tensor.matmul(out=acc[:], lhsT=ones[:], rhs=gate_rows[:, r, :], start=True, stop=True)

@@ -24,6 +24,7 @@ SLOTS = E * C
 BLOCKS = N // P
 
 COARSE = ((0, 24), (24, 48), (48, 64))
+HALF = T // 2
 VECTOR_SHARE = (352, 128, 0, 0)
 SPLIT = 2
 PLANES = 2
@@ -92,7 +93,7 @@ def tile_routed_moe_kernel(tc, xT, w_words, w_scales, gate, offs, pos1, pos2, ou
 
         for a in range(PASSES):
             cut = VECTOR_SHARE[a]
-            for lo, hi, on_vector in ((0, cut, True), (cut, T, False)):
+            for lo, hi, on_vector in ((0, min(cut, HALF), True), (HALF, max(cut, HALF), True), (cut, T, False)):
                 if lo < hi:
                     dst = grouped[a][:, lo:hi, :].rearrange("p (c i) t -> p c t i", i=4)
                     src = raw[a][:, :, lo:hi].rearrange("p t (c i) -> p c t i", i=4)
@@ -108,11 +109,11 @@ def tile_routed_moe_kernel(tc, xT, w_words, w_scales, gate, offs, pos1, pos2, ou
             nc.tensor.matmul(out=acc[:], lhsT=ones[:], rhs=gate_rows[:, r, :], start=True, stop=True)
             nc.scalar.copy(out=gates[r][:], in_=acc[:])
 
-        def quantise(a):
+        def quantise(a, lo=0, hi=T):
             nc.vector.quantize_mx(
-                out=tok_words[a][:].bitcast(FP8X4),
-                scales=tok_scales[4 * a : P, :],
-                in_=grouped[a][:].rearrange("p w j -> p (w j)"),
+                out=tok_words[a][:, lo:hi].bitcast(FP8X4),
+                scales=tok_scales[4 * a : P, lo:hi],
+                in_=grouped[a][:, lo:hi, :].rearrange("p w j -> p (w j)"),
             )
 
         def gather_words(a, cols):
@@ -129,7 +130,8 @@ def tile_routed_moe_kernel(tc, xT, w_words, w_scales, gate, offs, pos1, pos2, ou
                 in_=tok_scales[:].indirect(offs_t[:, lo:hi]),
             )
 
-        quantise(0)
+        quantise(0, 0, HALF)
+        quantise(0, HALF, T)
         for a in range(PASSES - 1):
             for cols in COARSE[:-1]:
                 gather_words(a, cols)
@@ -158,7 +160,7 @@ def tile_routed_moe_kernel(tc, xT, w_words, w_scales, gate, offs, pos1, pos2, ou
                     start=(a == 0),
                     stop=(a == PASSES - 1),
                 )
-            if (e, b) == (E - 1, 0):
+            if (e, b) == (E - 2, 0):
                 nc.vector.tensor_copy(out=y[b][:, slots], in_=acc[:])
             else:
                 nc.scalar.copy(out=y[b][:, slots], in_=acc[:])

@@ -25,7 +25,8 @@ BLOCKS = N // P
 
 COARSE = ((0, 24), (24, 48), (48, 64))
 HALF = T // 2
-VECTOR_SHARE = (352, 128, 0, 0)
+ROW_CUTS = (((0, 2), (2, 4)), ((0, 4),), ((0, 4),), ((0, 4),))
+VECTOR_SHARE = (320, 64, 0, 0)
 SPLIT = 2
 PLANES = 2
 
@@ -65,10 +66,9 @@ def tile_routed_moe_kernel(tc, xT, w_words, w_scales, gate, offs, pos1, pos2, ou
         make_identity(nc, ident[:])
 
         for a in range(PASSES):
-            nc.sync.dma_start(
-                out=raw[a][:],
-                in_=xT[a * K_PASS : (a + 1) * K_PASS, :].rearrange("(p j) w -> p j w", j=PACK),
-            )
+            rows = xT[a * K_PASS : (a + 1) * K_PASS, :].rearrange("(p j) w -> p j w", j=PACK)
+            for lo, hi in ROW_CUTS[a]:
+                nc.sync.dma_start(out=raw[a][:, lo:hi, :], in_=rows[:, lo:hi, :])
             if a == 0:
                 nc.sync.dma_start(offs_t[:], offs)
         nc.sync.dma_start(out=gate_rows[0:1, :, :], in_=gate[:, 0:1, :].rearrange("r o t -> o r t"))
@@ -93,14 +93,15 @@ def tile_routed_moe_kernel(tc, xT, w_words, w_scales, gate, offs, pos1, pos2, ou
 
         for a in range(PASSES):
             cut = VECTOR_SHARE[a]
-            for lo, hi, on_vector in ((0, min(cut, HALF), True), (HALF, max(cut, HALF), True), (cut, T, False)):
-                if lo < hi:
-                    dst = grouped[a][:, lo:hi, :].rearrange("p (c i) t -> p c t i", i=4)
-                    src = raw[a][:, :, lo:hi].rearrange("p t (c i) -> p c t i", i=4)
-                    if on_vector:
-                        nc.vector.tensor_copy(out=dst, in_=src)
-                    else:
-                        nc.scalar.copy(out=dst, in_=src)
+            for r_lo, r_hi in ROW_CUTS[a]:
+                for lo, hi, on_vector in ((0, min(cut, HALF), True), (HALF, max(cut, HALF), True), (cut, T, False)):
+                    if lo < hi:
+                        dst = grouped[a][:, lo:hi, r_lo:r_hi].rearrange("p (c i) t -> p c t i", i=4)
+                        src = raw[a][:, r_lo:r_hi, lo:hi].rearrange("p t (c i) -> p c t i", i=4)
+                        if on_vector:
+                            nc.vector.tensor_copy(out=dst, in_=src)
+                        else:
+                            nc.scalar.copy(out=dst, in_=src)
 
         ones = keep.tile([P, P], F32, name="ones", tag="late")
         nc.gpsimd.memset(ones[:], 1.0)

@@ -42,8 +42,8 @@ def tile_routed_moe_kernel(tc, xT, w_words, w_scales, gate, offs, pos1, pos2, ou
         pos1_t = lists.tile([P, T // 16], U16, name="pos1_t")
         pos2_t = lists.tile([P, T // 16], U16, name="pos2_t")
 
-        raw = [keep.tile([P, PACK, T], F32, name="raw%d" % a, tag="late" if a == PASSES - 1 else "raw%d" % a) for a in range(PASSES)]
-        grouped = [keep.tile([P, T, PACK], BF16, name="grouped%d" % a, align_bytes=64) for a in range(PASSES)]
+        raw = [keep.tile([P, PACK, T], F32, name="raw%d" % a) for a in range(PASSES)]
+        grouped = [keep.tile([P, T, PACK], BF16, name="grouped%d" % a, tag="late" if a == PASSES - 1 else "grouped%d" % a, align_bytes=64) for a in range(PASSES)]
         tok_words = [keep.tile([P, T], U32, name="tok_words%d" % a, align_bytes=64) for a in range(PASSES)]
         tok_scales = keep.tile([P, T], U8, name="tok_scales", align_bytes=64)
         slot_words = keep.tile([P, PASSES, SLOTS], U32, name="slot_words", align_bytes=64)
@@ -103,12 +103,14 @@ def tile_routed_moe_kernel(tc, xT, w_words, w_scales, gate, offs, pos1, pos2, ou
                         else:
                             nc.scalar.copy(out=dst, in_=src)
 
-        ones = keep.tile([P, P], F32, name="ones", tag="late")
-        nc.gpsimd.memset(ones[:], 1.0)
-        for r in range(2):
+        def spread_gate(r, ones):
+            nc.gpsimd.memset(ones[:], 1.0)
             acc = psum.tile([P, T], F32)
             nc.tensor.matmul(out=acc[:], lhsT=ones[:], rhs=gate_rows[:, r, :], start=True, stop=True)
             nc.scalar.copy(out=gates[r][:], in_=acc[:])
+
+        ones_early = keep.tile([P, P], F32, name="ones_early")
+        spread_gate(0, ones_early)
 
         def quantise(a, lo=0, hi=T):
             nc.vector.quantize_mx(
@@ -145,6 +147,9 @@ def tile_routed_moe_kernel(tc, xT, w_words, w_scales, gate, offs, pos1, pos2, ou
             gather_scales(cols)
         for cols in COARSE:
             gather_words(PASSES - 1, cols)
+
+        ones_late = keep.tile([P, P], F32, name="ones_late", tag="late", align_bytes=64)
+        spread_gate(1, ones_late)
 
         order = [(e, b) for b in range(BLOCKS) for e in range(E)]
         for e, b in order:

from contextlib import ExitStack

import concourse.mybir as mybir
from concourse.masks import make_identity

K, T, E, C, N = 2048, 512, 8, 128, 256
FLOPS = 2 * K * N * E * C

F32 = mybir.dt.float32
BF16 = mybir.dt.bfloat16
I32 = mybir.dt.int32
U32 = mybir.dt.uint32
U16 = mybir.dt.uint16
U8 = mybir.dt.uint8
FP8X4 = mybir.dt.float8_e4m3fn_x4
MULT = mybir.AluOpType.mult
ADD = mybir.AluOpType.add

P = 128
PACK = 4
K_PASS = P * PACK
PASSES = K // K_PASS
SLOTS = E * C
BLOCKS = N // P

COARSE = ((0, 24), (24, 48), (48, 64))
HALF = T // 2
ROW_CUTS = (((0, 2), (2, 4)), ((0, 4),), ((0, 4),), ((0, 4),))
VECTOR_SHARE = (320, 64, 0, 0)
SPLIT = 2
PLANES = 2


def tile_routed_moe_kernel(tc, xT, w_words, w_scales, gate, offs, pos1, pos2, out):
    nc = tc.nc
    with ExitStack() as ctx:
        lists = ctx.enter_context(tc.tile_pool(name="lists", bufs=1))
        keep = ctx.enter_context(tc.tile_pool(name="keep", bufs=1))
        psum = ctx.enter_context(tc.psum_pool(name="psum", bufs=8))

        offs_t = lists.tile([P, SLOTS // 16], U16, name="offs_t")
        pos1_t = lists.tile([P, T // 16], U16, name="pos1_t")
        pos2_t = lists.tile([P, T // 16], U16, name="pos2_t")

        raw = [keep.tile([P, PACK, T], F32, name="raw%d" % a) for a in range(PASSES)]
        grouped = [keep.tile([P, T, PACK], BF16, name="grouped%d" % a, tag="late" if a == PASSES - 1 else "grouped%d" % a, align_bytes=64) for a in range(PASSES)]
        tok_words = [keep.tile([P, T], U32, name="tok_words%d" % a, align_bytes=64) for a in range(PASSES)]
        tok_scales = keep.tile([P, T], U8, name="tok_scales", align_bytes=64)
        slot_words = keep.tile([P, PASSES, SLOTS], U32, name="slot_words", align_bytes=64)
        slot_scales = keep.tile([P, SLOTS], U8, name="slot_scales", align_bytes=64)
        wt_words = [keep.tile([P, PASSES, N], I32, name="wt_words%d" % e, align_bytes=64) for e in range(E)]
        wt_scales = keep.tile([P, E * PASSES // PLANES, N], U8, name="wt_scales", align_bytes=64)
        gate_rows = keep.tile([P, 2, T], F32, name="gate_rows")
        gates = [keep.tile([P, T], F32, name="gate%d" % r) for r in range(2)]
        y = [keep.tile([P, SLOTS], F32, name="y%d" % b) for b in range(BLOCKS)]

        warm_in = keep.tile([P, 1], F32, name="warm_in")
        warm_out = keep.tile([P, 1], F32, name="warm_out")
        nc.vector.memset(warm_in[:], 0.0)
        nc.scalar.copy(out=warm_out[:], in_=warm_in[:])
        nc.gpsimd.memset(tok_scales[:], 0)
        nc.vector.memset(gate_rows[:], 0.0)
        nc.vector.memset(wt_scales[:].rearrange("p g n -> p (g n)").bitcast(I32), 0)

        ident = keep.tile([P, P], F32, name="ident")
        make_identity(nc, ident[:])

        for a in range(PASSES):
            rows = xT[a * K_PASS : (a + 1) * K_PASS, :].rearrange("(p j) w -> p j w", j=PACK)
            for lo, hi in ROW_CUTS[a]:
                nc.sync.dma_start(out=raw[a][:, lo:hi, :], in_=rows[:, lo:hi, :])
            if a == 0:
                nc.sync.dma_start(offs_t[:], offs)
        nc.sync.dma_start(out=gate_rows[0:1, :, :], in_=gate[:, 0:1, :].rearrange("r o t -> o r t"))
        scale_rows = w_scales.rearrange("e (c j) (q r) n -> j r q (e c) n", j=PLANES, r=4)
        for j in range(PLANES):
            for r in range(4):
                nc.sync.dma_start(out=wt_scales[4 * j + r : P : 32, :, :].bitcast(I32), in_=scale_rows[j, r].bitcast(I32))
        for e in range(E - SPLIT):
            nc.sync.dma_start(
                out=wt_words[e][:],
                in_=w_words[e].rearrange("a p n r -> p a (n r)").bitcast(I32),
            )
            if e == 1:
                nc.sync.dma_start(pos1_t[:], pos1)
                nc.sync.dma_start(pos2_t[:], pos2)
        for b in range(BLOCKS):
            for e in range(E - SPLIT, E):
                nc.sync.dma_start(
                    out=wt_words[e][:, :, b * P : (b + 1) * P],
                    in_=w_words[e].rearrange("a p n r -> p a (n r)")[:, :, 4 * b * P : 4 * (b + 1) * P].bitcast(I32),
                )

        for a in range(PASSES):
            cut = VECTOR_SHARE[a]
            for r_lo, r_hi in ROW_CUTS[a]:
                for lo, hi, on_vector in ((0, min(cut, HALF), True), (HALF, max(cut, HALF), True), (cut, T, False)):
                    if lo < hi:
                        dst = grouped[a][:, lo:hi, r_lo:r_hi].rearrange("p (c i) t -> p c t i", i=4)
                        src = raw[a][:, r_lo:r_hi, lo:hi].rearrange("p t (c i) -> p c t i", i=4)
                        if on_vector:
                            nc.vector.tensor_copy(out=dst, in_=src)
                        else:
                            nc.scalar.copy(out=dst, in_=src)

        def spread_gate(r, ones):
            nc.gpsimd.memset(ones[:], 1.0)
            acc = psum.tile([P, T], F32)
            nc.tensor.matmul(out=acc[:], lhsT=ones[:], rhs=gate_rows[:, r, :], start=True, stop=True)
            nc.scalar.copy(out=gates[r][:], in_=acc[:])

        ones_early = keep.tile([P, P], F32, name="ones_early")
        spread_gate(0, ones_early)

        def quantise(a, lo=0, hi=T):
            nc.vector.quantize_mx(
                out=tok_words[a][:, lo:hi].bitcast(FP8X4),
                scales=tok_scales[4 * a : P, lo:hi],
                in_=grouped[a][:, lo:hi, :].rearrange("p w j -> p (w j)"),
            )

        def gather_words(a, cols):
            lo, hi = cols
            nc.vector.tensor_copy(
                out=slot_words[:, a, 16 * lo : 16 * hi],
                in_=tok_words[a][:].indirect(offs_t[:, lo:hi]),
            )

        def gather_scales(cols):
            lo, hi = cols
            nc.vector.tensor_copy(
                out=slot_scales[:, 16 * lo : 16 * hi],
                in_=tok_scales[:].indirect(offs_t[:, lo:hi]),
            )

        quantise(0, 0, HALF)
        quantise(0, HALF, T)
        for a in range(PASSES - 1):
            for cols in COARSE[:-1]:
                gather_words(a, cols)
            if a >= 1:
                quantise(a + 1)
            gather_words(a, COARSE[-1])
            if a < 1:
                quantise(a + 1)
        for cols in COARSE:
            gather_scales(cols)
        for cols in COARSE:
            gather_words(PASSES - 1, cols)

        ones_late = keep.tile([P, P], F32, name="ones_late", tag="late", align_bytes=64)
        spread_gate(1, ones_late)

        order = [(e, b) for b in range(BLOCKS) for e in range(E)]
        for e, b in order:
            slots = slice(e * C, (e + 1) * C)
            feats = slice(b * P, (b + 1) * P)
            acc = psum.tile([P, C], F32)
            for a in range(PASSES):
                nc.tensor.matmul_mx(
                    out=acc[:],
                    lhsT=wt_words[e][:, a, feats].bitcast(FP8X4),
                    lhsT_scale=wt_scales[4 * (a % PLANES) : P, (e * PASSES + a) // PLANES, feats],
                    rhs=slot_words[:, a, slots].bitcast(FP8X4),
                    rhs_scale=slot_scales[4 * a : P, slots],
                    start=(a == 0),
                    stop=(a == PASSES - 1),
                )
            if (e, b) == (E - 2, 0):
                nc.vector.tensor_copy(out=y[b][:, slots], in_=acc[:])
            else:
                nc.scalar.copy(out=y[b][:, slots], in_=acc[:])

        first = [keep.tile([P, T], F32, name="first%d" % b) for b in range(BLOCKS)]
        second = [keep.tile([P, T], F32, name="second%d" % b) for b in range(BLOCKS)]
        total = [keep.tile([P, T], F32, name="total%d" % b) for b in range(BLOCKS)]

        nc.vector.tensor_tensor(out=first[0][:], in0=y[0][:].indirect(pos1_t[:]), in1=gates[0][:], op=MULT)
        nc.vector.tensor_tensor(out=second[0][:], in0=y[0][:].indirect(pos2_t[:]), in1=gates[1][:], op=MULT)
        acc = psum.tile([P, T], F32)
        nc.tensor.matmul(out=acc[:], lhsT=ident[:], rhs=first[0][:], start=True, stop=False)
        nc.tensor.matmul(out=acc[:], lhsT=ident[:], rhs=second[0][:], start=False, stop=True)
        nc.scalar.copy(out=total[0][:], in_=acc[:])
        nc.sync.dma_start(out=out[0:P, :], in_=total[0][:])

        nc.vector.tensor_tensor(out=first[1][:], in0=y[1][:].indirect(pos1_t[:]), in1=gates[0][:], op=MULT)
        halves = ((0, T // 2), (T // 2, T))
        for lo, hi in halves:
            nc.vector.tensor_tensor(
                out=second[1][:, lo:hi], in0=y[1][:].indirect(pos2_t[:, lo // 16 : hi // 16]), in1=gates[1][:, lo:hi], op=MULT
            )
        for lo, hi in halves:
            nc.vector.tensor_tensor(out=total[1][:, lo:hi], in0=first[1][:, lo:hi], in1=second[1][:, lo:hi], op=ADD)
            nc.sync.dma_start(out=out[P : 2 * P, lo:hi], in_=total[1][:, lo:hi])
